import numpy as np
import ml_dtypes


def mxq(x, axis, fmt="e4m3"):
    dtype, down = {"e4m3": (ml_dtypes.float8_e4m3fn, 7), "e5m2": (ml_dtypes.float8_e5m2, 14)}[fmt]
    v = np.moveaxis(np.asarray(x, np.float32).astype(ml_dtypes.bfloat16).astype(np.float64), axis, -1)
    blocks = v.reshape(v.shape[:-1] + (-1, 32))
    amax = np.abs(blocks).max(-1, keepdims=True)
    byte = np.maximum(np.where(amax > 0, np.frexp(amax)[1] - 1 + 127, 0) - down, 1)
    scale = np.exp2(byte - 127.0)
    codes = (blocks / scale).astype(np.float32).astype(dtype).astype(np.float64)
    return np.moveaxis((codes * scale).reshape(v.shape), -1, axis)


WIDE = False


def mx_kscale(k):
    if not WIDE:
        return np.ones(k)
    levels = np.array([10, -10, 5, -5, 0])
    if k % 512:
        return np.exp2(np.random.permutation(np.resize(levels, k // 32))).repeat(32)
    a = np.empty((k // 512, 16))
    for p in range(k // 512):
        a[p, :8] = np.random.permutation(np.resize(levels, 8))
        for g in range(8):
            far = levels[np.abs(levels - a[p, g]) >= 10]
            a[p, g + 8] = far[np.random.randint(len(far))]
    return np.exp2(a.ravel()).repeat(32)


BF16 = ml_dtypes.bfloat16


def bf(x):
    return np.asarray(x, np.float32).astype(BF16)


def f64(x):
    return np.asarray(x).astype(np.float64)


E2M1 = np.array([0.0, 0.5, 1.0, 1.5, 2.0, 3.0, 4.0, 6.0, -0.0, -0.5, -1.0, -1.5, -2.0, -3.0, -4.0, -6.0])


def pack_weight(w, fmt):
    k, n = w.shape
    w = f64(bf(w)).reshape(k // 32, 32, n)
    amax = np.abs(w).max(1)
    if fmt == "e4m3":
        byte = np.frexp(amax)[1] - 1 + 127 - 7
    else:
        mant, ex = np.frexp(amax / 6.0)
        byte = np.where(mant > 0.5, ex, ex - 1) + 127
    byte = np.clip(np.where(amax > 0, byte, 1), 1, 254)
    scaled = (w * np.exp2(127.0 - byte)[:, None, :]).reshape(k, n).astype(np.float32)
    by_word = np.ascontiguousarray(scaled.reshape(k // 512, 128, 4, n).transpose(0, 1, 3, 2))
    if fmt == "e4m3":
        words = by_word.astype(ml_dtypes.float8_e4m3fn).view(np.uint8)
    else:
        c = by_word.astype(ml_dtypes.float4_e2m1fn).view(np.uint8) & 0xF
        words = c[..., 0::2] | (c[..., 1::2] << 4)
    return np.ascontiguousarray(words), np.ascontiguousarray(byte.astype(np.uint8).reshape(k // 512, 16, n))


def unpack_weight(words, scales, fmt):
    g, p, n, _ = words.shape
    if fmt == "e4m3":
        vals = np.ascontiguousarray(words).view(ml_dtypes.float8_e4m3fn).astype(np.float64)
    else:
        nib = np.empty((g, p, n, 4), np.uint8)
        nib[..., 0::2] = words & 0xF
        nib[..., 1::2] = words >> 4
        vals = E2M1[nib]
    vals = vals * np.repeat(np.exp2(scales.astype(np.float64) - 127.0), 8, axis=1)[..., None]
    return vals.transpose(0, 1, 3, 2).reshape(g * 512, n)
def pack4(w):
    words, scales = pack_weight(w, "e2m1")
    return words.reshape(words.shape[0], 128, -1), scales


def unpack4(words, scales):
    return unpack_weight(words.reshape(words.shape[0], 128, -1, 2), scales, "e2m1")


def planes(Y):
    n, m = Y.shape
    b = f64(bf(Y)).reshape(n // 32, 32, m)
    amax = np.abs(b).max(1)
    byte = np.clip(np.where(amax > 0, np.frexp(amax)[1] - 1 + 127 - 7, 1), 1, 254)
    codes = (b * np.exp2(127.0 - byte)[:, None, :]).reshape(n, m).astype(np.float32).astype(ml_dtypes.float8_e4m3fn).view(np.uint8)
    words = codes.reshape(n // 512, 128, 4, m).transpose(0, 1, 3, 2)
    return np.ascontiguousarray(words), np.ascontiguousarray(byte.astype(np.uint8).reshape(n // 512, 16, m))


T, D, L = 1024, 1024, 4096
COL_SPREAD = 0.6
MEAN_STD = 0.3
BIAS_STD = 0.3
THETA_MID, THETA_SPREAD = 0.6, 0.3


def setup_inputs():
    s = mx_kscale(D)
    mean = MEAN_STD * np.random.randn(D)
    x = (mean + np.random.randn(T, D)) * s
    b_dec = mean * s
    col = np.exp(COL_SPREAD * np.random.randn(L))
    w_enc = np.random.randn(D, L) / np.sqrt(D) * col / s[:, None]
    w_enc_words, w_enc_scales = pack4(w_enc)
    b_enc = BIAS_STD * np.random.randn(L)
    theta = THETA_MID * np.exp(THETA_SPREAD * np.random.randn(L))
    return {"x": bf(x), "b_dec": bf(b_dec), "w_enc_words": w_enc_words,
            "w_enc_scales": w_enc_scales, "b_enc": bf(b_enc), "theta": bf(theta)}


def reference(x, b_dec, w_enc_words, w_enc_scales, b_enc, theta):
    xc = f64(x) - f64(b_dec)
    h = mxq(xc, 1, "e4m3") @ unpack4(w_enc_words, w_enc_scales)
    u = h + f64(b_enc)
    gate = 1.0 / (1.0 + np.exp(f64(theta) - u))
    y = u * gate
    Y = y.T
    words, scales = planes(Y)
    return y, words, scales

@@ -1,0 +1,297 @@
+from contextlib import ExitStack
+
+import concourse.mybir as mybir
+from concourse.masks import make_identity
+
+T, D, L = 1024, 1024, 4096
+FLOPS = 2 * T * D * L
+
+F32 = mybir.dt.float32
+BF16 = mybir.dt.bfloat16
+I32 = mybir.dt.int32
+U8 = mybir.dt.uint8
+FP8X4 = mybir.dt.float8_e4m3fn_x4
+FP4X4 = mybir.dt.float4_e2m1fn_x4
+ALU = mybir.AluOpType
+ACT = mybir.ActivationFunctionType
+
+P = 128
+PACK = 4
+SPAN = P * PACK
+PASSES = D // SPAN
+GROUPS = L // SPAN
+HALVES = T // SPAN
+W_CHUNKS = [(0, 1), (1, 2), (2, 4), (4, 8)]
+S_CHUNKS = [(0, 2), (2, 8)]
+UNITS = [(0, 0), (1, 0), (0, 1), (1, 1)] + [(g, h) for g in range(2, GROUPS) for h in range(HALVES)]
+V_COPIES = [0, 0, 0, 1, 1, 1, 1, 1, 1, 1, 1, 1, 1, 2, 2, 2]
+LATE = 13
+MM0 = [(0, 0), (1, 0), (0, 1), (1, 1), (2, 0), (2, 1), (3, 0), (3, 1)]
+SCALAR_TOKENS = [0, 64, 32, 32, 32, 32, 32, 32, 32, 32, 32, 32, 32, 32, 32, 0]
+
+
+def tile_sae_smooth_jumprelu_encode_g4_kernel(
+    tc, x, b_dec, w_enc_words, w_enc_scales, b_enc, theta, out_0, out_1, out_2
+):
+    nc = tc.nc
+    with ExitStack() as ctx:
+        keep = ctx.enter_context(tc.tile_pool(name="keep", bufs=1))
+        work = ctx.enter_context(tc.tile_pool(name="work", bufs=3))
+        psum = ctx.enter_context(tc.psum_pool(name="psum", bufs=1))
+        ctx.enter_context(tc.manual_schedule())
+
+        ident = keep.tile([P, P], F32, name="ident")
+        vec_rows = keep.tile([P, SPAN], BF16, name="vec_rows")
+        s_raw = keep.tile([P, PASSES, L], U8, name="s_raw", align_bytes=64)
+        w_raw = [keep.tile([P, PASSES, 2 * SPAN * (b - a)], U8, name="w_raw%d" % a, align_bytes=64) for a, b in W_CHUNKS]
+        x_raw = {(h, k): keep.tile([P, PACK, SPAN], BF16, name="x_raw%d%d" % (h, k)) for h in range(HALVES) for k in range(PASSES)}
+        x_c = {hk: keep.tile([P, SPAN, PACK], BF16, name="x_c%d%d" % hk, align_bytes=64) for hk in x_raw if hk != (1, 1)}
+        x_c[1, 1] = work.tile([P, SPAN, PACK], BF16, name="y_bf", bufs=1, align_bytes=64)
+        x_codes = {hk: keep.tile([P, SPAN], I32, name="x_codes%d%d" % hk, align_bytes=64) for hk in x_raw}
+        x_scales = {hk: keep.tile([P, SPAN], U8, name="x_scales%d%d" % hk, align_bytes=64) for hk in x_raw}
+        w_codes = [keep.tile([P, PASSES, 2 * SPAN], U8, name="w_codes%d" % g, align_bytes=64) for g in range(GROUPS)]
+        w_scales = [keep.tile([P, PASSES, SPAN], U8, name="w_scales%d" % g, align_bytes=64) for g in range(GROUPS)]
+        y_scales = keep.tile([P, GROUPS // 4, T], U8, name="y_scales", align_bytes=64)
+        bdec = keep.tile([P, PASSES, 16], BF16, name="bdec")
+        vecs = keep.tile([P, 2 * GROUPS, PACK], F32, name="vecs")
+        shift = keep.tile([P, GROUPS, PACK], F32, name="shift")
+
+        w_hbm = w_enc_words.bitcast(I32).rearrange("k p c -> p k c")
+        s_hbm = w_enc_scales.bitcast(I32).rearrange("k q c -> q k c")
+        words_hbm = out_1.rearrange("g p m t -> g p (m t)").bitcast(I32)
+        scales_hbm = out_2.bitcast(I32)
+
+        def load_x(h, k, j0=0, j1=PACK):
+            rows = x[h * SPAN + j0 * P : h * SPAN + j1 * P, k * SPAN : (k + 1) * SPAN]
+            nc.sync.dma_start(out=x_raw[h, k][:, j0:j1, :], in_=rows.rearrange("(j p) d -> p j d", p=P))
+
+        def load_w(c):
+            a, b = W_CHUNKS[c]
+            nc.sync.dma_start(out=w_raw[c][:].bitcast(I32), in_=w_hbm[:, :, a * SPAN // 2 : b * SPAN // 2])
+
+        def load_s(c):
+            a, b = S_CHUNKS[c]
+            cols = slice(a * SPAN // 4, b * SPAN // 4)
+            for q in range(4):
+                nc.sync.dma_start(out=s_raw[:].bitcast(I32)[32 * q : 32 * q + 4, :, cols], in_=s_hbm[4 * q : 4 * q + 4, :, cols])
+
+        def zero_s(c):
+            a, b = S_CHUNKS[c]
+            nc.vector.memset(s_raw[:].bitcast(I32)[:, :, a * SPAN // 4 : b * SPAN // 4], 0)
+
+        def permute_w(g, k):
+            c = [i for i, (a, b) in enumerate(W_CHUNKS) if a <= g < b][0]
+            off = (g - W_CHUNKS[c][0]) * 2 * SPAN
+            nc.vector.tensor_copy(
+                out=w_codes[g][:, k, :].rearrange("p (t m e) -> p t m e", t=PACK, e=2),
+                in_=w_raw[c][:, k, off : off + 2 * SPAN].rearrange("p (m t e) -> p t m e", t=PACK, e=2),
+            )
+            nc.vector.tensor_copy(
+                out=w_scales[g][:, k, :].rearrange("p (t m) -> p t m", t=PACK),
+                in_=s_raw[:, k, g * SPAN : (g + 1) * SPAN].rearrange("p (m t) -> p t m", t=PACK),
+            )
+
+        turn_banks = {}
+
+        def turn_x(h, k, pairs=(0, 1)):
+            words = x_raw[h, k][:].bitcast(F32)
+            for pair in pairs:
+                bank = psum.tile([P, 2, 2 * P], F32, name="turn", tag="turn%d" % (2 * k + pair))
+                turn_banks[h, k, pair] = bank
+                for jj in range(2):
+                    for u in range(2):
+                        nc.tensor.transpose(bank[:, u, jj * P : (jj + 1) * P], words[:, 2 * pair + jj, u : 2 * P : 2], ident[:])
+
+        def centre_x(h, k, pairs=(0, 1)):
+            for pair in pairs:
+                bank = turn_banks[h, k, pair]
+                nc.vector.tensor_tensor(
+                    out=x_c[h, k][:, pair * 2 * P : (pair + 1) * 2 * P, :].rearrange("p m (u e) -> p m u e", e=2),
+                    in0=bank[:].bitcast(BF16).rearrange("p u (m e) -> p m u e", e=2),
+                    in1=bdec[:, k, 0:PACK].rearrange("p (u e) -> p u e", e=2).unsqueeze(1).to_broadcast([P, 2 * P, 2, 2]),
+                    op=ALU.subtract,
+                )
+
+        def quantise_x(h, k):
+            nc.vector.quantize_mx(out=x_codes[h, k][:].bitcast(FP8X4), scales=x_scales[h, k][:], in_=x_c[h, k][:].rearrange("p m t -> p (m t)"))
+
+        acc = {}
+
+        def matmul(i, t, k):
+            g, h = UNITS[i]
+            if k == 0:
+                acc[i, t] = psum.tile([P, SPAN], F32, name="acc", tag="acc%d" % t)
+            nc.tensor.matmul_mx(
+                out=acc[i, t][:],
+                lhsT=w_codes[g][:, k, 2 * P * t : 2 * P * (t + 1)].bitcast(FP4X4),
+                lhsT_scale=w_scales[g][:, k, P * t : P * (t + 1)],
+                rhs=x_codes[h, k][:].bitcast(FP8X4),
+                rhs_scale=x_scales[h, k][:],
+                start=(k == 0),
+                stop=(k == PASSES - 1),
+            )
+
+        y_lat, y_bf, y_tok, y_banks = {}, {}, {}, {}
+
+        def activate(i, t):
+            g, h = UNITS[i]
+            if t == 0:
+                y_lat[i] = work.tile([P, PACK, SPAN], F32, name="y_lat")
+            gate = work.tile([P, SPAN], F32, name="gate", bufs=4)
+            nc.scalar.activation(out=gate[:], in_=acc[i, t][:], func=ACT.Sigmoid, bias=shift[:, g, t : t + 1])
+            nc.vector.scalar_tensor_tensor(
+                out=y_lat[i][:, t, :], in0=acc[i, t][:], scalar=vecs[:, g, t : t + 1], in1=gate[:], op0=ALU.add, op1=ALU.mult
+            )
+
+        def round_y(i):
+            y_bf[i] = work.tile([P, SPAN, PACK], BF16, name="y_bf", bufs=1, align_bytes=64)
+            src = y_lat[i][:].rearrange("p t m -> p m t")
+            if i == len(UNITS) - 1:
+                nc.vector.tensor_copy(out=y_bf[i][:], in_=src)
+            else:
+                n = SPAN - SCALAR_TOKENS[i]
+                if n > 0:
+                    nc.gpsimd.tensor_scalar(out=y_bf[i][:, :n], in0=src[:, :n], scalar1=1.0, scalar2=1.0, op0=ALU.mult, op1=ALU.mult)
+
+        def round_y_rest(i):
+            n = SPAN - SCALAR_TOKENS[i]
+            if n < SPAN:
+                nc.scalar.copy(out=y_bf[i][:, n:], in_=y_lat[i][:].rearrange("p t m -> p m t")[:, n:])
+
+        def quantise_y(i):
+            g, h = UNITS[i]
+            codes = work.tile([P, SPAN], I32, name="y_codes", align_bytes=64)
+            tokens = slice(h * SPAN, (h + 1) * SPAN)
+            nc.vector.quantize_mx(
+                out=codes[:].bitcast(FP8X4), scales=y_scales[4 * (g % 4) :, g // 4, tokens], in_=y_bf[i][:].rearrange("p m t -> p (m t)")
+            )
+            nc.sync.dma_start(out=words_hbm[g, :, tokens], in_=codes[:])
+            if i == 7:
+                store_scales(0)
+
+        def store_scales(s):
+            for q in range(4):
+                nc.sync.dma_start(
+                    out=scales_hbm[4 * s : 4 * s + 4, 4 * q : 4 * q + 4, :],
+                    in_=y_scales[:].bitcast(I32)[32 * q : 32 * q + 16, s, :],
+                )
+
+        def turn_y(i, j):
+            bank = psum.tile([P, PACK, P], F32, name="turn", tag="turn%d" % j)
+            y_banks[i, j] = bank
+            for t in range(PACK):
+                nc.tensor.transpose(bank[:, t, :], y_lat[i][:, t, j * P : (j + 1) * P], ident[:])
+
+        def copy_y(i, j, on_vector):
+            if j == 0:
+                y_tok[i] = work.tile([P, PACK, SPAN], F32, name="y_tok")
+            dst = y_tok[i][:, j, :].rearrange("p (m t) -> p m t", t=PACK)
+            src = y_banks[i, j][:].rearrange("p t m -> p m t")
+            if on_vector:
+                nc.vector.tensor_copy(out=dst, in_=src)
+            else:
+                nc.scalar.copy(out=dst, in_=src)
+
+        def store_y(i, j0, j1):
+            g, h = UNITS[i]
+            rows = out_0[h * SPAN + j0 * P : h * SPAN + j1 * P, g * SPAN : (g + 1) * SPAN]
+            nc.sync.dma_start(out=rows.rearrange("(j p) n -> p j n", p=P), in_=y_tok[i][:, j0:j1, :])
+
+        zero_s(0)
+        nc.vector.memset(vec_rows[:], 0.0)
+        make_identity(nc, ident[:])
+        zero_s(1)
+        load_x(0, 0, 0, 2)
+        load_w(0)
+        nc.sync.dma_start(out=bdec[:, :, 0:PACK], in_=b_dec.rearrange("(k p t) -> p k t", p=P, t=PACK))
+        load_x(0, 0, 2, 4)
+        load_s(0)
+        load_x(0, 1, 0, 2)
+        load_w(1)
+        load_x(0, 1, 2, 4)
+        nc.sync.dma_start(out=vec_rows[0:GROUPS, :], in_=b_enc.rearrange("(r c) -> r c", c=SPAN))
+        nc.sync.dma_start(out=vec_rows[GROUPS : 2 * GROUPS, :], in_=theta.rearrange("(r c) -> r c", c=SPAN))
+        load_x(1, 0)
+        load_x(1, 1)
+        load_s(1)
+        load_w(2)
+        load_w(3)
+
+        turn_x(0, 0)
+        turn_x(0, 1)
+        vec_bank = psum.tile([P, 2, P], F32, name="vec_bank", tag="acc3")
+        for u in range(2):
+            nc.tensor.transpose(vec_bank[:, u, :], vec_rows[:].bitcast(F32)[:, u : 2 * P : 2], ident[:])
+        vec_cols = vec_bank[:].bitcast(BF16).rearrange("p u (r e) -> p r u e", e=2)
+        nc.scalar.copy(out=vecs[:].rearrange("p r (u e) -> p r u e", e=2), in_=vec_cols[:, 0 : 2 * GROUPS])
+        permute_w(0, 0)
+        centre_x(0, 0, (0,))
+        permute_w(0, 1)
+        centre_x(0, 0, (1,))
+        permute_w(1, 0)
+        quantise_x(0, 0)
+        centre_x(0, 1)
+        nc.vector.tensor_tensor(out=shift[:], in0=vecs[:, 0:GROUPS, :], in1=vecs[:, GROUPS:, :], op=ALU.subtract)
+        quantise_x(0, 1)
+        for t, k in MM0:
+            matmul(0, t, k)
+        permute_w(1, 1)
+        turn_x(1, 0)
+
+        last = len(UNITS) - 1
+        for i in range(len(UNITS)):
+            for t in (0, 1):
+                activate(i, t)
+                if i == 1 and t == 0:
+                    quantise_x(1, 1)
+                    round_y(0)
+                if i < last:
+                    matmul(i + 1, t, 0)
+                    matmul(i + 1, t, 1)
+            if i > 0:
+                round_y_rest(i - 1)
+            if 1 < i < LATE:
+                copy_y(i - 2, 2, False)
+                copy_y(i - 2, 3, V_COPIES[i] > 0)
+                store_y(i - 2, 2, PACK)
+            if i >= LATE:
+                copy_y(i - 1, 0, False)
+                copy_y(i - 1, 1, V_COPIES[i] > 0)
+                store_y(i - 1, 0, 2)
+            if i == 0:
+                turn_x(1, 1)
+                centre_x(1, 0)
+            else:
+                turn_y(i - 1, 2)
+                turn_y(i - 1, 3)
+            for t in (2, 3):
+                activate(i, t)
+                if i < last:
+                    matmul(i + 1, t, 0)
+                    matmul(i + 1, t, 1)
+            if i == 0:
+                quantise_x(1, 0)
+                centre_x(1, 1)
+            elif (i + 3) // 2 < GROUPS:
+                permute_w((i + 3) // 2, (i + 3) % 2)
+            if i > 0:
+                quantise_y(i - 1)
+                round_y(i)
+            if 0 < i < LATE:
+                copy_y(i - 1, 0, False)
+                copy_y(i - 1, 1, V_COPIES[i] > 1)
+                store_y(i - 1, 0, 2)
+            if i >= LATE - 1:
+                copy_y(i - 1, 2, False)
+                copy_y(i - 1, 3, V_COPIES[i] > 1)
+                store_y(i - 1, 2, PACK)
+            turn_y(i, 0)
+            turn_y(i, 1)
+        turn_y(last, 2)
+        turn_y(last, 3)
+        for j in range(PACK):
+            if j == 3:
+                quantise_y(last)
+            copy_y(last, j, False)
+            store_y(last, j, j + 1)
+        store_scales(1)

@@ -21,13 +21,15 @@ SPAN = P * PACK
 PASSES = D // SPAN
 GROUPS = L // SPAN
 HALVES = T // SPAN
-W_CHUNKS = [(0, 1), (1, 2), (2, 4), (4, 8)]
-S_CHUNKS = [(0, 2), (2, 8)]
+TILES = SPAN // P
+QUADRANTS = P // 32
+SHARED = 4
+
+W_CHUNKS = [(0, 1), (1, 3), (3, 5), (5, 8)]
+HEAD_GROUPS = 3
 UNITS = [(0, 0), (1, 0), (0, 1), (1, 1)] + [(g, h) for g in range(2, GROUPS) for h in range(HALVES)]
-V_COPIES = [0, 0, 0, 1, 1, 1, 1, 1, 1, 1, 1, 1, 1, 2, 2, 2]
-LATE = 13
-MM0 = [(0, 0), (1, 0), (0, 1), (1, 1), (2, 0), (2, 1), (3, 0), (3, 1)]
-SCALAR_TOKENS = [0, 64, 32, 32, 32, 32, 32, 32, 32, 32, 32, 32, 32, 32, 32, 0]
+LAST = len(UNITS) - 1
+FIRST_MATMULS = [(0, 0), (1, 0), (0, 1), (1, 1), (2, 0), (2, 1), (3, 0), (3, 1)]
 
 
 def tile_sae_smooth_jumprelu_encode_g4_kernel(
@@ -36,32 +38,33 @@ def tile_sae_smooth_jumprelu_encode_g4_kernel(
     nc = tc.nc
     with ExitStack() as ctx:
         keep = ctx.enter_context(tc.tile_pool(name="keep", bufs=1))
-        work = ctx.enter_context(tc.tile_pool(name="work", bufs=3))
+        work = ctx.enter_context(tc.tile_pool(name="work", bufs=1))
         psum = ctx.enter_context(tc.psum_pool(name="psum", bufs=1))
         ctx.enter_context(tc.manual_schedule())
 
+        x_parts = [(h, k) for h in range(HALVES) for k in range(PASSES)]
         ident = keep.tile([P, P], F32, name="ident")
         vec_rows = keep.tile([P, SPAN], BF16, name="vec_rows")
-        s_raw = keep.tile([P, PASSES, L], U8, name="s_raw", align_bytes=64)
+        s_raw = keep.tile([P, L // 4], U8, name="s_raw", align_bytes=64)
+        s_sorted = keep.tile([P, L // 4], U8, name="s_sorted", align_bytes=64)
         w_raw = [keep.tile([P, PASSES, 2 * SPAN * (b - a)], U8, name="w_raw%d" % a, align_bytes=64) for a, b in W_CHUNKS]
-        x_raw = {(h, k): keep.tile([P, PACK, SPAN], BF16, name="x_raw%d%d" % (h, k)) for h in range(HALVES) for k in range(PASSES)}
-        x_c = {hk: keep.tile([P, SPAN, PACK], BF16, name="x_c%d%d" % hk, align_bytes=64) for hk in x_raw if hk != (1, 1)}
-        x_c[1, 1] = work.tile([P, SPAN, PACK], BF16, name="y_bf", bufs=1, align_bytes=64)
-        x_codes = {hk: keep.tile([P, SPAN], I32, name="x_codes%d%d" % hk, align_bytes=64) for hk in x_raw}
-        x_scales = {hk: keep.tile([P, SPAN], U8, name="x_scales%d%d" % hk, align_bytes=64) for hk in x_raw}
+        x_raw = {hk: keep.tile([P, TILES, SPAN], BF16, name="x_raw%d%d" % hk) for hk in x_parts}
+        x_centred = {hk: keep.tile([P, SPAN, PACK], BF16, name="x_centred%d%d" % hk, align_bytes=64) for hk in x_parts}
+        x_codes = {hk: keep.tile([P, SPAN], I32, name="x_codes%d%d" % hk, align_bytes=64) for hk in x_parts}
+        x_scales = {hk: keep.tile([P, SPAN], U8, name="x_scales%d%d" % hk, align_bytes=64) for hk in x_parts}
         w_codes = [keep.tile([P, PASSES, 2 * SPAN], U8, name="w_codes%d" % g, align_bytes=64) for g in range(GROUPS)]
-        w_scales = [keep.tile([P, PASSES, SPAN], U8, name="w_scales%d" % g, align_bytes=64) for g in range(GROUPS)]
-        y_scales = keep.tile([P, GROUPS // 4, T], U8, name="y_scales", align_bytes=64)
+        w_scales = keep.tile([P, PASSES, L], U8, name="w_scales", align_bytes=64)
+        y_scales = keep.tile([P, GROUPS // SHARED, T], U8, name="y_scales", align_bytes=64)
         bdec = keep.tile([P, PASSES, 16], BF16, name="bdec")
         vecs = keep.tile([P, 2 * GROUPS, PACK], F32, name="vecs")
         shift = keep.tile([P, GROUPS, PACK], F32, name="shift")
 
         w_hbm = w_enc_words.bitcast(I32).rearrange("k p c -> p k c")
-        s_hbm = w_enc_scales.bitcast(I32).rearrange("k q c -> q k c")
+        s_hbm = w_enc_scales.bitcast(I32).rearrange("k q (c w) -> (k q c) w", c=4)
         words_hbm = out_1.rearrange("g p m t -> g p (m t)").bitcast(I32)
         scales_hbm = out_2.bitcast(I32)
 
-        def load_x(h, k, j0=0, j1=PACK):
+        def load_x(h, k, j0, j1):
             rows = x[h * SPAN + j0 * P : h * SPAN + j1 * P, k * SPAN : (k + 1) * SPAN]
             nc.sync.dma_start(out=x_raw[h, k][:, j0:j1, :], in_=rows.rearrange("(j p) d -> p j d", p=P))
 
@@ -69,53 +72,49 @@ def tile_sae_smooth_jumprelu_encode_g4_kernel(
             a, b = W_CHUNKS[c]
             nc.sync.dma_start(out=w_raw[c][:].bitcast(I32), in_=w_hbm[:, :, a * SPAN // 2 : b * SPAN // 2])
 
-        def load_s(c):
-            a, b = S_CHUNKS[c]
-            cols = slice(a * SPAN // 4, b * SPAN // 4)
-            for q in range(4):
-                nc.sync.dma_start(out=s_raw[:].bitcast(I32)[32 * q : 32 * q + 4, :, cols], in_=s_hbm[4 * q : 4 * q + 4, :, cols])
+        def spread_w_scales(k):
+            for q in range(QUADRANTS):
+                first = 64 * k + 16 * q
+                nc.sync.dma_start(
+                    out=w_scales[:].bitcast(I32)[32 * q : 32 * q + 4, k, :],
+                    in_=s_sorted[:].bitcast(I32)[first : first + 16, :],
+                )
 
-        def zero_s(c):
-            a, b = S_CHUNKS[c]
-            nc.vector.memset(s_raw[:].bitcast(I32)[:, :, a * SPAN // 4 : b * SPAN // 4], 0)
-
-        def permute_w(g, k):
-            c = [i for i, (a, b) in enumerate(W_CHUNKS) if a <= g < b][0]
+        def sort_w(g, k):
+            c = [n for n, (a, b) in enumerate(W_CHUNKS) if a <= g < b][0]
             off = (g - W_CHUNKS[c][0]) * 2 * SPAN
             nc.vector.tensor_copy(
                 out=w_codes[g][:, k, :].rearrange("p (t m e) -> p t m e", t=PACK, e=2),
                 in_=w_raw[c][:, k, off : off + 2 * SPAN].rearrange("p (m t e) -> p t m e", t=PACK, e=2),
             )
-            nc.vector.tensor_copy(
-                out=w_scales[g][:, k, :].rearrange("p (t m) -> p t m", t=PACK),
-                in_=s_raw[:, k, g * SPAN : (g + 1) * SPAN].rearrange("p (m t) -> p t m", t=PACK),
-            )
 
-        turn_banks = {}
+        x_banks = {}
 
-        def turn_x(h, k, pairs=(0, 1)):
+        def turn_x(h, k):
             words = x_raw[h, k][:].bitcast(F32)
-            for pair in pairs:
-                bank = psum.tile([P, 2, 2 * P], F32, name="turn", tag="turn%d" % (2 * k + pair))
-                turn_banks[h, k, pair] = bank
+            for pair in range(2):
+                bank = psum.tile([P, 2, 2 * P], F32, name="x_bank", tag="turn%d" % (2 * k + pair))
+                x_banks[h, k, pair] = bank
                 for jj in range(2):
                     for u in range(2):
                         nc.tensor.transpose(bank[:, u, jj * P : (jj + 1) * P], words[:, 2 * pair + jj, u : 2 * P : 2], ident[:])
 
-        def centre_x(h, k, pairs=(0, 1)):
-            for pair in pairs:
-                bank = turn_banks[h, k, pair]
-                nc.vector.tensor_tensor(
-                    out=x_c[h, k][:, pair * 2 * P : (pair + 1) * 2 * P, :].rearrange("p m (u e) -> p m u e", e=2),
-                    in0=bank[:].bitcast(BF16).rearrange("p u (m e) -> p m u e", e=2),
-                    in1=bdec[:, k, 0:PACK].rearrange("p (u e) -> p u e", e=2).unsqueeze(1).to_broadcast([P, 2 * P, 2, 2]),
-                    op=ALU.subtract,
-                )
+        def centre_x(h, k, pair):
+            nc.vector.tensor_tensor(
+                out=x_centred[h, k][:, pair * 2 * P : (pair + 1) * 2 * P, :].rearrange("p m (u e) -> p m u e", e=2),
+                in0=x_banks[h, k, pair][:].bitcast(BF16).rearrange("p u (m e) -> p m u e", e=2),
+                in1=bdec[:, k, 0:PACK].rearrange("p (u e) -> p u e", e=2).unsqueeze(1).to_broadcast([P, 2 * P, 2, 2]),
+                op=ALU.subtract,
+            )
 
         def quantise_x(h, k):
-            nc.vector.quantize_mx(out=x_codes[h, k][:].bitcast(FP8X4), scales=x_scales[h, k][:], in_=x_c[h, k][:].rearrange("p m t -> p (m t)"))
+            nc.vector.quantize_mx(
+                out=x_codes[h, k][:].bitcast(FP8X4),
+                scales=x_scales[h, k][:],
+                in_=x_centred[h, k][:].rearrange("p m t -> p (m t)"),
+            )
 
-        acc = {}
+        acc, y_lat, y_bf, y_tok, y_banks = {}, {}, {}, {}, {}
 
         def matmul(i, t, k):
             g, h = UNITS[i]
@@ -124,174 +123,177 @@ def tile_sae_smooth_jumprelu_encode_g4_kernel(
             nc.tensor.matmul_mx(
                 out=acc[i, t][:],
                 lhsT=w_codes[g][:, k, 2 * P * t : 2 * P * (t + 1)].bitcast(FP4X4),
-                lhsT_scale=w_scales[g][:, k, P * t : P * (t + 1)],
+                lhsT_scale=w_scales[:, k, g * SPAN + P * t : g * SPAN + P * (t + 1)],
                 rhs=x_codes[h, k][:].bitcast(FP8X4),
                 rhs_scale=x_scales[h, k][:],
                 start=(k == 0),
                 stop=(k == PASSES - 1),
             )
 
-        y_lat, y_bf, y_tok, y_banks = {}, {}, {}, {}
-
         def activate(i, t):
-            g, h = UNITS[i]
+            g = UNITS[i][0]
             if t == 0:
-                y_lat[i] = work.tile([P, PACK, SPAN], F32, name="y_lat")
-            gate = work.tile([P, SPAN], F32, name="gate", bufs=4)
+                y_lat[i] = work.tile([P, PACK, SPAN], F32, name="y_lat", bufs=4)
+            gate = work.tile([P, SPAN], F32, name="gate", bufs=PACK)
             nc.scalar.activation(out=gate[:], in_=acc[i, t][:], func=ACT.Sigmoid, bias=shift[:, g, t : t + 1])
             nc.vector.scalar_tensor_tensor(
                 out=y_lat[i][:, t, :], in0=acc[i, t][:], scalar=vecs[:, g, t : t + 1], in1=gate[:], op0=ALU.add, op1=ALU.mult
             )
 
-        def round_y(i):
-            y_bf[i] = work.tile([P, SPAN, PACK], BF16, name="y_bf", bufs=1, align_bytes=64)
-            src = y_lat[i][:].rearrange("p t m -> p m t")
-            if i == len(UNITS) - 1:
-                nc.vector.tensor_copy(out=y_bf[i][:], in_=src)
-            else:
-                n = SPAN - SCALAR_TOKENS[i]
-                if n > 0:
-                    nc.gpsimd.tensor_scalar(out=y_bf[i][:, :n], in0=src[:, :n], scalar1=1.0, scalar2=1.0, op0=ALU.mult, op1=ALU.mult)
+        def interleaved(i, m0, m1):
+            dst = y_bf[i][:, m0:m1, :].rearrange("p (c e) t -> p c t e", e=2)
+            src = y_lat[i][:, :, m0:m1].rearrange("p t (c e) -> p c t e", e=2)
+            return dst, src
 
-        def round_y_rest(i):
-            n = SPAN - SCALAR_TOKENS[i]
-            if n < SPAN:
-                nc.scalar.copy(out=y_bf[i][:, n:], in_=y_lat[i][:].rearrange("p t m -> p m t")[:, n:])
+        def round_y_on_gpsimd(i, tokens):
+            y_bf[i] = work.tile([P, SPAN, PACK], BF16, name="y_bf", align_bytes=64)
+            dst, src = interleaved(i, 0, tokens)
+            nc.gpsimd.tensor_scalar(out=dst, in0=src, scalar1=1.0, scalar2=1.0, op0=ALU.mult, op1=ALU.mult)
 
         def quantise_y(i):
             g, h = UNITS[i]
-            codes = work.tile([P, SPAN], I32, name="y_codes", align_bytes=64)
+            codes = work.tile([P, SPAN], I32, name="y_codes", bufs=len(UNITS), align_bytes=64)
             tokens = slice(h * SPAN, (h + 1) * SPAN)
             nc.vector.quantize_mx(
-                out=codes[:].bitcast(FP8X4), scales=y_scales[4 * (g % 4) :, g // 4, tokens], in_=y_bf[i][:].rearrange("p m t -> p (m t)")
+                out=codes[:].bitcast(FP8X4),
+                scales=y_scales[4 * (g % SHARED) :, g // SHARED, tokens],
+                in_=y_bf[i][:].rearrange("p m t -> p (m t)"),
             )
             nc.sync.dma_start(out=words_hbm[g, :, tokens], in_=codes[:])
-            if i == 7:
-                store_scales(0)
 
-        def store_scales(s):
-            for q in range(4):
+        def store_y_scales(s):
+            for q in range(QUADRANTS):
                 nc.sync.dma_start(
-                    out=scales_hbm[4 * s : 4 * s + 4, 4 * q : 4 * q + 4, :],
-                    in_=y_scales[:].bitcast(I32)[32 * q : 32 * q + 16, s, :],
+                    out=scales_hbm[SHARED * s : SHARED * (s + 1), 4 * q : 4 * q + 4, :],
+                    in_=y_scales[:].bitcast(I32)[32 * q : 32 * q + 4 * SHARED, s, :],
                 )
 
-        def turn_y(i, j):
-            bank = psum.tile([P, PACK, P], F32, name="turn", tag="turn%d" % j)
-            y_banks[i, j] = bank
-            for t in range(PACK):
-                nc.tensor.transpose(bank[:, t, :], y_lat[i][:, t, j * P : (j + 1) * P], ident[:])
+        def turn_y(i, banks):
+            for j in range(TILES):
+                y_banks[i, j] = psum.tile([P, PACK, P], F32, name="y_bank", tag="%s%d" % (banks, j))
+                for t in range(PACK):
+                    nc.tensor.transpose(y_banks[i, j][:, t, :], y_lat[i][:, t, j * P : (j + 1) * P], ident[:])
 
-        def copy_y(i, j, on_vector):
+        def copy_y(i, j, copy):
             if j == 0:
-                y_tok[i] = work.tile([P, PACK, SPAN], F32, name="y_tok")
-            dst = y_tok[i][:, j, :].rearrange("p (m t) -> p m t", t=PACK)
-            src = y_banks[i, j][:].rearrange("p t m -> p m t")
-            if on_vector:
-                nc.vector.tensor_copy(out=dst, in_=src)
-            else:
-                nc.scalar.copy(out=dst, in_=src)
+                y_tok[i] = work.tile([P, TILES, SPAN], F32, name="y_tok", bufs=8)
+            copy(out=y_tok[i][:, j, :].rearrange("p (m t) -> p m t", t=PACK), in_=y_banks[i, j][:].rearrange("p t m -> p m t"))
 
         def store_y(i, j0, j1):
             g, h = UNITS[i]
             rows = out_0[h * SPAN + j0 * P : h * SPAN + j1 * P, g * SPAN : (g + 1) * SPAN]
             nc.sync.dma_start(out=rows.rearrange("(j p) n -> p j n", p=P), in_=y_tok[i][:, j0:j1, :])
 
-        zero_s(0)
+        on_scalar, on_vector = nc.scalar.copy, nc.vector.tensor_copy
+
         nc.vector.memset(vec_rows[:], 0.0)
         make_identity(nc, ident[:])
-        zero_s(1)
+        nc.vector.memset(w_scales[:].bitcast(I32), 0)
+        nc.sync.dma_start(out=s_raw[:].bitcast(I32), in_=s_hbm)
         load_x(0, 0, 0, 2)
         load_w(0)
         nc.sync.dma_start(out=bdec[:, :, 0:PACK], in_=b_dec.rearrange("(k p t) -> p k t", p=P, t=PACK))
         load_x(0, 0, 2, 4)
-        load_s(0)
         load_x(0, 1, 0, 2)
-        load_w(1)
         load_x(0, 1, 2, 4)
-        nc.sync.dma_start(out=vec_rows[0:GROUPS, :], in_=b_enc.rearrange("(r c) -> r c", c=SPAN))
-        nc.sync.dma_start(out=vec_rows[GROUPS : 2 * GROUPS, :], in_=theta.rearrange("(r c) -> r c", c=SPAN))
-        load_x(1, 0)
-        load_x(1, 1)
-        load_s(1)
+        load_w(1)
+        nc.vector.tensor_copy(
+            out=s_sorted[:].rearrange("p (g t m) -> p g t m", g=2, t=PACK),
+            in_=s_raw[:].rearrange("p (g m t) -> p g t m", g=2, t=PACK),
+        )
+        spread_w_scales(0)
+        nc.sync.dma_start(out=vec_rows[0:GROUPS, :], in_=b_enc.rearrange("(g c) -> g c", c=SPAN))
+        nc.sync.dma_start(out=vec_rows[GROUPS : 2 * GROUPS, :], in_=theta.rearrange("(g c) -> g c", c=SPAN))
+        spread_w_scales(1)
+        load_x(1, 0, 0, TILES)
+        load_x(1, 1, 0, TILES)
         load_w(2)
         load_w(3)
 
         turn_x(0, 0)
         turn_x(0, 1)
-        vec_bank = psum.tile([P, 2, P], F32, name="vec_bank", tag="acc3")
+        vec_bank = psum.tile([P, 2, P], F32, name="vec_bank", tag="acc%d" % (PACK - 1))
         for u in range(2):
             nc.tensor.transpose(vec_bank[:, u, :], vec_rows[:].bitcast(F32)[:, u : 2 * P : 2], ident[:])
-        vec_cols = vec_bank[:].bitcast(BF16).rearrange("p u (r e) -> p r u e", e=2)
-        nc.scalar.copy(out=vecs[:].rearrange("p r (u e) -> p r u e", e=2), in_=vec_cols[:, 0 : 2 * GROUPS])
-        permute_w(0, 0)
-        centre_x(0, 0, (0,))
-        permute_w(0, 1)
-        centre_x(0, 0, (1,))
-        permute_w(1, 0)
+        nc.scalar.copy(
+            out=vecs[:].rearrange("p r (u e) -> p r u e", e=2),
+            in_=vec_bank[:].bitcast(BF16).rearrange("p u (r e) -> p r u e", e=2)[:, 0 : 2 * GROUPS],
+        )
+        sort_w(0, 0)
+        centre_x(0, 0, 0)
+        sort_w(0, 1)
+        centre_x(0, 0, 1)
+        centre_x(0, 1, 0)
         quantise_x(0, 0)
-        centre_x(0, 1)
+        centre_x(0, 1, 1)
         nc.vector.tensor_tensor(out=shift[:], in0=vecs[:, 0:GROUPS, :], in1=vecs[:, GROUPS:, :], op=ALU.subtract)
         quantise_x(0, 1)
-        for t, k in MM0:
+        for t, k in FIRST_MATMULS:
             matmul(0, t, k)
-        permute_w(1, 1)
+        sort_w(1, 0)
+        sort_w(1, 1)
+        sort_w(2, 0)
         turn_x(1, 0)
 
-        last = len(UNITS) - 1
-        for i in range(len(UNITS)):
-            for t in (0, 1):
+        for t in range(PACK):
+            activate(0, t)
+            if t == 1:
+                sort_w(2, 1)
+                centre_x(1, 0, 0)
+                centre_x(1, 0, 1)
+            matmul(1, t, 0)
+            matmul(1, t, 1)
+            if t == 1:
+                turn_x(1, 1)
+        quantise_x(1, 0)
+        centre_x(1, 1, 0)
+        centre_x(1, 1, 1)
+        round_y_on_gpsimd(0, SPAN // 2)
+        turn_y(0, "turn")
+
+        for i in range(1, LAST):
+            for t in range(PACK):
                 activate(i, t)
                 if i == 1 and t == 0:
                     quantise_x(1, 1)
-                    round_y(0)
-                if i < last:
-                    matmul(i + 1, t, 0)
-                    matmul(i + 1, t, 1)
-            if i > 0:
-                round_y_rest(i - 1)
-            if 1 < i < LATE:
-                copy_y(i - 2, 2, False)
-                copy_y(i - 2, 3, V_COPIES[i] > 0)
-                store_y(i - 2, 2, PACK)
-            if i >= LATE:
-                copy_y(i - 1, 0, False)
-                copy_y(i - 1, 1, V_COPIES[i] > 0)
-                store_y(i - 1, 0, 2)
-            if i == 0:
-                turn_x(1, 1)
-                centre_x(1, 0)
-            else:
-                turn_y(i - 1, 2)
-                turn_y(i - 1, 3)
-            for t in (2, 3):
-                activate(i, t)
-                if i < last:
-                    matmul(i + 1, t, 0)
-                    matmul(i + 1, t, 1)
-            if i == 0:
-                quantise_x(1, 0)
-                centre_x(1, 1)
-            elif (i + 3) // 2 < GROUPS:
-                permute_w((i + 3) // 2, (i + 3) % 2)
-            if i > 0:
-                quantise_y(i - 1)
-                round_y(i)
-            if 0 < i < LATE:
-                copy_y(i - 1, 0, False)
-                copy_y(i - 1, 1, V_COPIES[i] > 1)
-                store_y(i - 1, 0, 2)
-            if i >= LATE - 1:
-                copy_y(i - 1, 2, False)
-                copy_y(i - 1, 3, V_COPIES[i] > 1)
-                store_y(i - 1, 2, PACK)
-            turn_y(i, 0)
-            turn_y(i, 1)
-        turn_y(last, 2)
-        turn_y(last, 3)
-        for j in range(PACK):
-            if j == 3:
-                quantise_y(last)
-            copy_y(last, j, False)
-            store_y(last, j, j + 1)
-        store_scales(1)
+                matmul(i + 1, t, 0)
+                matmul(i + 1, t, 1)
+                if i == 1 and t == 1:
+                    dst, src = interleaved(0, SPAN // 2, SPAN)
+                    nc.scalar.copy(out=dst, in_=src)
+            copy_y(i - 1, 0, on_scalar)
+            copy_y(i - 1, 1, on_scalar)
+            store_y(i - 1, 0, 2)
+            quantise_y(i - 1)
+            if UNITS[i - 1] == (SHARED - 1, HALVES - 1):
+                store_y_scales(0)
+            g_next, k_next = divmod(i + 3, PASSES)
+            if HEAD_GROUPS <= g_next < GROUPS:
+                sort_w(g_next, k_next)
+            round_y_on_gpsimd(i, SPAN)
+            copy_y(i - 1, 2, on_scalar)
+            copy_y(i - 1, 3, on_vector)
+            store_y(i - 1, 2, 4)
+            turn_y(i, "turn")
+
+        activate(LAST, 0)
+        activate(LAST, 1)
+        copy_y(LAST - 1, 0, on_scalar)
+        copy_y(LAST - 1, 1, on_vector)
+        store_y(LAST - 1, 0, 2)
+        activate(LAST, 2)
+        activate(LAST, 3)
+        for j in (2, 3):
+            copy_y(LAST - 1, j, on_scalar)
+            store_y(LAST - 1, j, j + 1)
+        quantise_y(LAST - 1)
+        turn_y(LAST, "acc")
+        y_bf[LAST] = keep.tile([P, SPAN, PACK], BF16, name="y_bf_last", align_bytes=64)
+        dst, src = interleaved(LAST, 0, SPAN)
+        nc.vector.tensor_copy(out=dst, in_=src)
+        for j in range(TILES):
+            if j == TILES - 1:
+                quantise_y(LAST)
+                store_y_scales(1)
+            copy_y(LAST, j, on_scalar)
+            store_y(LAST, j, j + 1)

from contextlib import ExitStack

import concourse.mybir as mybir
from concourse.masks import make_identity

T, D, L = 1024, 1024, 4096
FLOPS = 2 * T * D * L

F32 = mybir.dt.float32
BF16 = mybir.dt.bfloat16
I32 = mybir.dt.int32
U8 = mybir.dt.uint8
FP8X4 = mybir.dt.float8_e4m3fn_x4
FP4X4 = mybir.dt.float4_e2m1fn_x4
ALU = mybir.AluOpType
ACT = mybir.ActivationFunctionType

P = 128
PACK = 4
SPAN = P * PACK
PASSES = D // SPAN
GROUPS = L // SPAN
HALVES = T // SPAN
TILES = SPAN // P
QUADRANTS = P // 32
SHARED = 4

W_CHUNKS = [(0, 1), (1, 3), (3, 5), (5, 8)]
HEAD_GROUPS = 3
UNITS = [(0, 0), (1, 0), (0, 1), (1, 1)] + [(g, h) for g in range(2, GROUPS) for h in range(HALVES)]
LAST = len(UNITS) - 1
FIRST_MATMULS = [(0, 0), (1, 0), (0, 1), (1, 1), (2, 0), (2, 1), (3, 0), (3, 1)]


def tile_sae_smooth_jumprelu_encode_g4_kernel(
    tc, x, b_dec, w_enc_words, w_enc_scales, b_enc, theta, out_0, out_1, out_2
):
    nc = tc.nc
    with ExitStack() as ctx:
        keep = ctx.enter_context(tc.tile_pool(name="keep", bufs=1))
        work = ctx.enter_context(tc.tile_pool(name="work", bufs=1))
        psum = ctx.enter_context(tc.psum_pool(name="psum", bufs=1))
        ctx.enter_context(tc.manual_schedule())

        x_parts = [(h, k) for h in range(HALVES) for k in range(PASSES)]
        ident = keep.tile([P, P], F32, name="ident")
        vec_rows = keep.tile([P, SPAN], BF16, name="vec_rows")
        s_raw = keep.tile([P, L // 4], U8, name="s_raw", align_bytes=64)
        s_sorted = keep.tile([P, L // 4], U8, name="s_sorted", align_bytes=64)
        w_raw = [keep.tile([P, PASSES, 2 * SPAN * (b - a)], U8, name="w_raw%d" % a, align_bytes=64) for a, b in W_CHUNKS]
        x_raw = {hk: keep.tile([P, TILES, SPAN], BF16, name="x_raw%d%d" % hk) for hk in x_parts}
        x_centred = {hk: keep.tile([P, SPAN, PACK], BF16, name="x_centred%d%d" % hk, align_bytes=64) for hk in x_parts}
        x_codes = {hk: keep.tile([P, SPAN], I32, name="x_codes%d%d" % hk, align_bytes=64) for hk in x_parts}
        x_scales = {hk: keep.tile([P, SPAN], U8, name="x_scales%d%d" % hk, align_bytes=64) for hk in x_parts}
        w_codes = [keep.tile([P, PASSES, 2 * SPAN], U8, name="w_codes%d" % g, align_bytes=64) for g in range(GROUPS)]
        w_scales = keep.tile([P, PASSES, L], U8, name="w_scales", align_bytes=64)
        y_scales = keep.tile([P, GROUPS // SHARED, T], U8, name="y_scales", align_bytes=64)
        bdec = keep.tile([P, PASSES, 16], BF16, name="bdec")
        vecs = keep.tile([P, 2 * GROUPS, PACK], F32, name="vecs")
        shift = keep.tile([P, GROUPS, PACK], F32, name="shift")

        w_hbm = w_enc_words.bitcast(I32).rearrange("k p c -> p k c")
        s_hbm = w_enc_scales.bitcast(I32).rearrange("k q (c w) -> (k q c) w", c=4)
        words_hbm = out_1.rearrange("g p m t -> g p (m t)").bitcast(I32)
        scales_hbm = out_2.bitcast(I32)

        def load_x(h, k, j0, j1):
            rows = x[h * SPAN + j0 * P : h * SPAN + j1 * P, k * SPAN : (k + 1) * SPAN]
            nc.sync.dma_start(out=x_raw[h, k][:, j0:j1, :], in_=rows.rearrange("(j p) d -> p j d", p=P))

        def load_w(c):
            a, b = W_CHUNKS[c]
            nc.sync.dma_start(out=w_raw[c][:].bitcast(I32), in_=w_hbm[:, :, a * SPAN // 2 : b * SPAN // 2])

        def spread_w_scales(k):
            for q in range(QUADRANTS):
                first = 64 * k + 16 * q
                nc.sync.dma_start(
                    out=w_scales[:].bitcast(I32)[32 * q : 32 * q + 4, k, :],
                    in_=s_sorted[:].bitcast(I32)[first : first + 16, :],
                )

        def sort_w(g, k):
            c = [n for n, (a, b) in enumerate(W_CHUNKS) if a <= g < b][0]
            off = (g - W_CHUNKS[c][0]) * 2 * SPAN
            nc.vector.tensor_copy(
                out=w_codes[g][:, k, :].rearrange("p (t m e) -> p t m e", t=PACK, e=2),
                in_=w_raw[c][:, k, off : off + 2 * SPAN].rearrange("p (m t e) -> p t m e", t=PACK, e=2),
            )

        x_banks = {}

        def turn_x(h, k):
            words = x_raw[h, k][:].bitcast(F32)
            for pair in range(2):
                bank = psum.tile([P, 2, 2 * P], F32, name="x_bank", tag="turn%d" % (2 * k + pair))
                x_banks[h, k, pair] = bank
                for jj in range(2):
                    for u in range(2):
                        nc.tensor.transpose(bank[:, u, jj * P : (jj + 1) * P], words[:, 2 * pair + jj, u : 2 * P : 2], ident[:])

        def centre_x(h, k, pair):
            nc.vector.tensor_tensor(
                out=x_centred[h, k][:, pair * 2 * P : (pair + 1) * 2 * P, :].rearrange("p m (u e) -> p m u e", e=2),
                in0=x_banks[h, k, pair][:].bitcast(BF16).rearrange("p u (m e) -> p m u e", e=2),
                in1=bdec[:, k, 0:PACK].rearrange("p (u e) -> p u e", e=2).unsqueeze(1).to_broadcast([P, 2 * P, 2, 2]),
                op=ALU.subtract,
            )

        def quantise_x(h, k):
            nc.vector.quantize_mx(
                out=x_codes[h, k][:].bitcast(FP8X4),
                scales=x_scales[h, k][:],
                in_=x_centred[h, k][:].rearrange("p m t -> p (m t)"),
            )

        acc, y_lat, y_bf, y_tok, y_banks = {}, {}, {}, {}, {}

        def matmul(i, t, k):
            g, h = UNITS[i]
            if k == 0:
                acc[i, t] = psum.tile([P, SPAN], F32, name="acc", tag="acc%d" % t)
            nc.tensor.matmul_mx(
                out=acc[i, t][:],
                lhsT=w_codes[g][:, k, 2 * P * t : 2 * P * (t + 1)].bitcast(FP4X4),
                lhsT_scale=w_scales[:, k, g * SPAN + P * t : g * SPAN + P * (t + 1)],
                rhs=x_codes[h, k][:].bitcast(FP8X4),
                rhs_scale=x_scales[h, k][:],
                start=(k == 0),
                stop=(k == PASSES - 1),
            )

        def activate(i, t):
            g = UNITS[i][0]
            if t == 0:
                y_lat[i] = work.tile([P, PACK, SPAN], F32, name="y_lat", bufs=4)
            gate = work.tile([P, SPAN], F32, name="gate", bufs=PACK)
            nc.scalar.activation(out=gate[:], in_=acc[i, t][:], func=ACT.Sigmoid, bias=shift[:, g, t : t + 1])
            nc.vector.scalar_tensor_tensor(
                out=y_lat[i][:, t, :], in0=acc[i, t][:], scalar=vecs[:, g, t : t + 1], in1=gate[:], op0=ALU.add, op1=ALU.mult
            )

        def interleaved(i, m0, m1):
            dst = y_bf[i][:, m0:m1, :].rearrange("p (c e) t -> p c t e", e=2)
            src = y_lat[i][:, :, m0:m1].rearrange("p t (c e) -> p c t e", e=2)
            return dst, src

        def round_y_on_gpsimd(i, tokens):
            y_bf[i] = work.tile([P, SPAN, PACK], BF16, name="y_bf", align_bytes=64)
            dst, src = interleaved(i, 0, tokens)
            nc.gpsimd.tensor_scalar(out=dst, in0=src, scalar1=1.0, scalar2=1.0, op0=ALU.mult, op1=ALU.mult)

        def quantise_y(i):
            g, h = UNITS[i]
            codes = work.tile([P, SPAN], I32, name="y_codes", bufs=len(UNITS), align_bytes=64)
            tokens = slice(h * SPAN, (h + 1) * SPAN)
            nc.vector.quantize_mx(
                out=codes[:].bitcast(FP8X4),
                scales=y_scales[4 * (g % SHARED) :, g // SHARED, tokens],
                in_=y_bf[i][:].rearrange("p m t -> p (m t)"),
            )
            nc.sync.dma_start(out=words_hbm[g, :, tokens], in_=codes[:])

        def store_y_scales(s):
            for q in range(QUADRANTS):
                nc.sync.dma_start(
                    out=scales_hbm[SHARED * s : SHARED * (s + 1), 4 * q : 4 * q + 4, :],
                    in_=y_scales[:].bitcast(I32)[32 * q : 32 * q + 4 * SHARED, s, :],
                )

        def turn_y(i, banks):
            for j in range(TILES):
                y_banks[i, j] = psum.tile([P, PACK, P], F32, name="y_bank", tag="%s%d" % (banks, j))
                for t in range(PACK):
                    nc.tensor.transpose(y_banks[i, j][:, t, :], y_lat[i][:, t, j * P : (j + 1) * P], ident[:])

        def copy_y(i, j, copy):
            if j == 0:
                y_tok[i] = work.tile([P, TILES, SPAN], F32, name="y_tok", bufs=8)
            copy(out=y_tok[i][:, j, :].rearrange("p (m t) -> p m t", t=PACK), in_=y_banks[i, j][:].rearrange("p t m -> p m t"))

        def store_y(i, j0, j1):
            g, h = UNITS[i]
            rows = out_0[h * SPAN + j0 * P : h * SPAN + j1 * P, g * SPAN : (g + 1) * SPAN]
            nc.sync.dma_start(out=rows.rearrange("(j p) n -> p j n", p=P), in_=y_tok[i][:, j0:j1, :])

        on_scalar, on_vector = nc.scalar.copy, nc.vector.tensor_copy

        nc.vector.memset(vec_rows[:], 0.0)
        make_identity(nc, ident[:])
        nc.vector.memset(w_scales[:].bitcast(I32), 0)
        nc.sync.dma_start(out=s_raw[:].bitcast(I32), in_=s_hbm)
        load_x(0, 0, 0, 2)
        load_w(0)
        nc.sync.dma_start(out=bdec[:, :, 0:PACK], in_=b_dec.rearrange("(k p t) -> p k t", p=P, t=PACK))
        load_x(0, 0, 2, 4)
        load_x(0, 1, 0, 2)
        load_x(0, 1, 2, 4)
        load_w(1)
        nc.vector.tensor_copy(
            out=s_sorted[:].rearrange("p (g t m) -> p g t m", g=2, t=PACK),
            in_=s_raw[:].rearrange("p (g m t) -> p g t m", g=2, t=PACK),
        )
        spread_w_scales(0)
        nc.sync.dma_start(out=vec_rows[0:GROUPS, :], in_=b_enc.rearrange("(g c) -> g c", c=SPAN))
        nc.sync.dma_start(out=vec_rows[GROUPS : 2 * GROUPS, :], in_=theta.rearrange("(g c) -> g c", c=SPAN))
        spread_w_scales(1)
        load_x(1, 0, 0, TILES)
        load_x(1, 1, 0, TILES)
        load_w(2)
        load_w(3)

        turn_x(0, 0)
        turn_x(0, 1)
        vec_bank = psum.tile([P, 2, P], F32, name="vec_bank", tag="acc%d" % (PACK - 1))
        for u in range(2):
            nc.tensor.transpose(vec_bank[:, u, :], vec_rows[:].bitcast(F32)[:, u : 2 * P : 2], ident[:])
        nc.scalar.copy(
            out=vecs[:].rearrange("p r (u e) -> p r u e", e=2),
            in_=vec_bank[:].bitcast(BF16).rearrange("p u (r e) -> p r u e", e=2)[:, 0 : 2 * GROUPS],
        )
        sort_w(0, 0)
        centre_x(0, 0, 0)
        sort_w(0, 1)
        centre_x(0, 0, 1)
        centre_x(0, 1, 0)
        quantise_x(0, 0)
        centre_x(0, 1, 1)
        nc.vector.tensor_tensor(out=shift[:], in0=vecs[:, 0:GROUPS, :], in1=vecs[:, GROUPS:, :], op=ALU.subtract)
        quantise_x(0, 1)
        for t, k in FIRST_MATMULS:
            matmul(0, t, k)
        sort_w(1, 0)
        sort_w(1, 1)
        sort_w(2, 0)
        turn_x(1, 0)

        for t in range(PACK):
            activate(0, t)
            if t == 1:
                sort_w(2, 1)
                centre_x(1, 0, 0)
                centre_x(1, 0, 1)
            matmul(1, t, 0)
            matmul(1, t, 1)
            if t == 1:
                turn_x(1, 1)
        quantise_x(1, 0)
        centre_x(1, 1, 0)
        centre_x(1, 1, 1)
        round_y_on_gpsimd(0, SPAN // 2)
        turn_y(0, "turn")

        for i in range(1, LAST):
            for t in range(PACK):
                activate(i, t)
                if i == 1 and t == 0:
                    quantise_x(1, 1)
                matmul(i + 1, t, 0)
                matmul(i + 1, t, 1)
                if i == 1 and t == 1:
                    dst, src = interleaved(0, SPAN // 2, SPAN)
                    nc.scalar.copy(out=dst, in_=src)
            copy_y(i - 1, 0, on_scalar)
            copy_y(i - 1, 1, on_scalar)
            store_y(i - 1, 0, 2)
            quantise_y(i - 1)
            if UNITS[i - 1] == (SHARED - 1, HALVES - 1):
                store_y_scales(0)
            g_next, k_next = divmod(i + 3, PASSES)
            if HEAD_GROUPS <= g_next < GROUPS:
                sort_w(g_next, k_next)
            round_y_on_gpsimd(i, SPAN)
            copy_y(i - 1, 2, on_scalar)
            copy_y(i - 1, 3, on_vector)
            store_y(i - 1, 2, 4)
            turn_y(i, "turn")

        activate(LAST, 0)
        activate(LAST, 1)
        copy_y(LAST - 1, 0, on_scalar)
        copy_y(LAST - 1, 1, on_vector)
        store_y(LAST - 1, 0, 2)
        activate(LAST, 2)
        activate(LAST, 3)
        for j in (2, 3):
            copy_y(LAST - 1, j, on_scalar)
            store_y(LAST - 1, j, j + 1)
        quantise_y(LAST - 1)
        turn_y(LAST, "acc")
        y_bf[LAST] = keep.tile([P, SPAN, PACK], BF16, name="y_bf_last", align_bytes=64)
        dst, src = interleaved(LAST, 0, SPAN)
        nc.vector.tensor_copy(out=dst, in_=src)
        for j in range(TILES):
            if j == TILES - 1:
                quantise_y(LAST)
                store_y_scales(1)
            copy_y(LAST, j, on_scalar)
            store_y(LAST, j, j + 1)
